import numpy as np
import ml_dtypes


def mxq(x, axis, fmt="e4m3"):
    dtype, down = {"e4m3": (ml_dtypes.float8_e4m3fn, 7), "e5m2": (ml_dtypes.float8_e5m2, 14)}[fmt]
    v = np.moveaxis(np.asarray(x, np.float32).astype(ml_dtypes.bfloat16).astype(np.float64), axis, -1)
    blocks = v.reshape(v.shape[:-1] + (-1, 32))
    amax = np.abs(blocks).max(-1, keepdims=True)
    byte = np.maximum(np.where(amax > 0, np.frexp(amax)[1] - 1 + 127, 0) - down, 1)
    scale = np.exp2(byte - 127.0)
    codes = (blocks / scale).astype(np.float32).astype(dtype).astype(np.float64)
    return np.moveaxis((codes * scale).reshape(v.shape), -1, axis)


WIDE = False


def mx_kscale(k):
    if not WIDE:
        return np.ones(k)
    levels = np.array([10, -10, 5, -5, 0])
    if k % 512:
        return np.exp2(np.random.permutation(np.resize(levels, k // 32))).repeat(32)
    a = np.empty((k // 512, 16))
    for p in range(k // 512):
        a[p, :8] = np.random.permutation(np.resize(levels, 8))
        for g in range(8):
            far = levels[np.abs(levels - a[p, g]) >= 10]
            a[p, g + 8] = far[np.random.randint(len(far))]
    return np.exp2(a.ravel()).repeat(32)


def f64(x):
    return np.asarray(x).astype(np.float64)


def striped(idx):
    return np.tile(idx.reshape(-1, 16).T, (8, 1)).astype(np.uint16)


def unstriped(offs):
    return offs[:16].T.reshape(-1).astype(np.int64)


E2M1 = np.array([0.0, 0.5, 1.0, 1.5, 2.0, 3.0, 4.0, 6.0, -0.0, -0.5, -1.0, -1.5, -2.0, -3.0, -4.0, -6.0])


def pack_weight(w, fmt):
    k, n = w.shape
    w = f64(np.asarray(w, np.float32).astype(ml_dtypes.bfloat16)).reshape(k // 32, 32, n)
    amax = np.abs(w).max(1)
    if fmt == "e4m3":
        byte = np.frexp(amax)[1] - 1 + 127 - 7
    else:
        mant, ex = np.frexp(amax / 6.0)
        byte = np.where(mant > 0.5, ex, ex - 1) + 127
    byte = np.clip(np.where(amax > 0, byte, 1), 1, 254)
    scaled = (w * np.exp2(127.0 - byte)[:, None, :]).reshape(k, n).astype(np.float32)
    by_word = np.ascontiguousarray(scaled.reshape(k // 512, 128, 4, n).transpose(0, 1, 3, 2))
    if fmt == "e4m3":
        words = by_word.astype(ml_dtypes.float8_e4m3fn).view(np.uint8)
    else:
        c = by_word.astype(ml_dtypes.float4_e2m1fn).view(np.uint8) & 0xF
        words = (c[..., 0::2] | (c[..., 1::2] << 4)).reshape(k // 512, 128, 2 * n)
    return np.ascontiguousarray(words), np.ascontiguousarray(byte.astype(np.uint8).reshape(k // 512, 16, n))


def unpack_weight(words, scales, fmt):
    g, _, n = scales.shape
    words = np.ascontiguousarray(words).reshape(g, 128, n, -1)
    if fmt == "e4m3":
        vals = words.view(ml_dtypes.float8_e4m3fn).astype(np.float64)
    else:
        nib = np.empty((g, 128, n, 4), np.uint8)
        nib[..., 0::2] = words & 0xF
        nib[..., 1::2] = words >> 4
        vals = E2M1[nib]
    vals = vals * np.repeat(np.exp2(scales.astype(np.float64) - 127.0), 8, axis=1)[..., None]
    return vals.transpose(0, 1, 3, 2).reshape(g * 512, n)


def gelu(v):
    return 0.5 * v * (1.0 + np.tanh(np.sqrt(2.0 / np.pi) * (v + 0.044715 * v**3)))


K, H, M, N, T, S, P = 1536, 1024, 512, 384, 2048, 1024, 512

def setup_inputs():
    n = np.random.standard_normal
    s = mx_kscale(K)[:, None]
    u = mx_kscale(H)[:, None]
    u2 = mx_kscale(M)[:, None]
    tab_words, tab_scales = pack_weight(n((K, T)) * s, "e4m3")
    w2_words, w2_scales = pack_weight(1.1 * n((H, M)) / np.sqrt(H) / u, "e2m1")
    w4_words, w4_scales = pack_weight(0.8 * n((H, N)) / np.sqrt(H) / u, "e4m3")
    return {
        "tab_words": tab_words, "tab_scales": tab_scales,
        "offs": striped(np.random.permutation(T)[:S]),
        "pos1": striped(np.random.permutation(S)[:P]),
        "pos2": striped(np.random.permutation(S)[:P]),
        "w1": (0.9 * n((K, H)) / np.sqrt(K) / s).astype(np.float32),
        "temp": np.random.uniform(0.4, 1.6, H).astype(np.float32),
        "lift": np.random.uniform(3.0, 7.0, H).astype(np.float32),
        "care": (n((H, P)) * u).astype(np.float32),
        "w2_words": w2_words, "w2_scales": w2_scales,
        "bias": (0.5 * n(M)).astype(np.float32),
        "gain": (np.random.uniform(0.7, 1.8, M) * u2[:, 0]).astype(np.float32),
        "w3": (n((M, N)) / np.sqrt(M) / u2).astype(np.float32),
        "w4_words": w4_words, "w4_scales": w4_scales,
    }

def reference(tab_words, tab_scales, offs, pos1, pos2, w1, temp, lift, care,
              w2_words, w2_scales, bias, gain, w3, w4_words, w4_scales):
    v = unpack_weight(tab_words, tab_scales, "e4m3")[:, unstriped(offs)]
    h = mxq(f64(w1), 0, "e4m3").T @ v
    top = h.max(axis=1)
    today = np.exp(f64(temp)[:, None] * (h[:, unstriped(pos1)] - top[:, None]))
    worst = np.maximum(f64(lift)[:, None] * today, h[:, unstriped(pos2)]) * f64(care)
    worst_m = mxq(worst, 0, "e4m3")
    w2 = unpack_weight(w2_words, w2_scales, "e2m1")
    first = w2.T @ worst_m
    bent = np.tanh(first + f64(bias)[:, None]) * f64(gain)[:, None]
    w4 = unpack_weight(w4_words, w4_scales, "e4m3")
    return mxq(f64(w3), 0, "e4m3").T @ mxq(bent, 0, "e4m3") + w4.T @ worst_m

@@ -1,0 +1,325 @@
+from contextlib import ExitStack
+
+import concourse.mybir as mybir
+
+K, H, M, N, T, S, J = 1536, 1024, 512, 384, 2048, 1024, 512
+FLOPS = 2 * (K * H * S + H * M * J + M * N * J + H * N * J)
+
+F32 = mybir.dt.float32
+BF16 = mybir.dt.bfloat16
+I32 = mybir.dt.int32
+U32 = mybir.dt.uint32
+U16 = mybir.dt.uint16
+U8 = mybir.dt.uint8
+FP8X4 = mybir.dt.float8_e4m3fn_x4
+FP4X4 = mybir.dt.float4_e2m1fn_x4
+ALU = mybir.AluOpType
+ACT = mybir.ActivationFunctionType
+
+P = 128
+PACK = 4
+PASS = P * PACK
+KP = K // PASS
+HP = H // PASS
+BANK = 512
+CH = 128
+NT = N // P
+
+
+def tile_list_wound_dressing_scores_kernel(
+    tc, tab_words, tab_scales, offs, pos1, pos2, w1, temp, lift, care,
+    w2_words, w2_scales, bias, gain, w3, w4_words, w4_scales, out,
+):
+    nc = tc.nc
+    with ExitStack() as ctx:
+        lists = ctx.enter_context(tc.tile_pool(name="lists", bufs=1))
+        keep = ctx.enter_context(tc.tile_pool(name="keep", bufs=1))
+        work = ctx.enter_context(tc.tile_pool(name="work", bufs=2))
+        psum = ctx.enter_context(tc.psum_pool(name="psum", bufs=2))
+
+        def kept(name, shape, dtype):
+            return keep.tile(shape, dtype, name=name, align_bytes=64)
+
+        offs_sb = lists.tile([P, S // 16], U16, name="offs_sb")
+        pos1_sb = lists.tile([P, J // 16], U16, name="pos1_sb")
+        pos2_sb = lists.tile([P, J // 16], U16, name="pos2_sb")
+
+        tab_sb = [kept("tab%d" % a, [P, T], U32) for a in range(KP)]
+        tab_sc = kept("tab_sc", [P, T], U8)
+        v_words = [kept("v_words%d" % a, [P, S], U32) for a in range(KP)]
+        v_sc = kept("v_sc", [P, S], U8)
+        half = PASS // 2
+        w1_raw = {}
+        for b in range(HP):
+            for a in range(KP):
+                for e in range(2):
+                    w1_raw[a, b, e] = kept("w1_raw%d%d%d" % (a, b, e), [P, PACK, half], F32)
+        w1_words = {(a, b): kept("w1_words%d%d" % (a, b), [P, PASS], U32) for a in range(KP) for b in range(HP)}
+        w1_sc = {(a, b): kept("w1_sc%d%d" % (a, b), [P, PASS], U8) for a in range(KP) for b in range(HP)}
+        temp_sb = kept("temp_sb", [P, HP * PACK], F32)
+        neg_temp = kept("neg_temp", [P, HP * PACK], F32)
+        lift_sb = kept("lift_sb", [P, HP * PACK], F32)
+        bias_sb = kept("bias_sb", [P, PACK], F32)
+        gain_sb = kept("gain_sb", [P, PACK], F32)
+        care_sb = [kept("care%d" % b, [P, PACK, J], F32) for b in range(HP)]
+        w2_raw = kept("w2_raw", [P, HP * 2 * M], U8)
+        w2_sb = kept("w2_sb", [P, HP * 2 * M], U8)
+        w2_sc_raw = kept("w2_sc_raw", [P, HP * M], U8)
+        w2_sc = kept("w2_sc", [P, HP * M], U8)
+        w4_sb = kept("w4_sb", [P, HP * N], U32)
+        w4_sc = kept("w4_sc", [P, HP * N], U8)
+        w3_raw = kept("w3_raw", [P, PACK, N], F32)
+        w3_bf = kept("w3_bf", [P, N * PACK], BF16)
+        w3_words = kept("w3_words", [P, N], U32)
+        w3_sc = kept("w3_sc", [P, N], U8)
+        larger = [kept("larger%d" % b, [P, PACK, J], F32) for b in range(HP)]
+        worst_bf = [kept("worst_bf%d" % b, [P, J * PACK], BF16) for b in range(HP)]
+        worst_words = [kept("worst_words%d" % b, [P, J], U32) for b in range(HP)]
+        worst_sc = [kept("worst_sc%d" % b, [P, J], U8) for b in range(HP)]
+
+        for plane in (tab_sc, w2_sc_raw, w4_sc):
+            nc.vector.memset(plane[:].bitcast(I32), 0)
+
+        def load_tab(a):
+            nc.sync.dma_start(out=tab_sb[a][:].bitcast(I32),
+                              in_=tab_words[a].rearrange("p t i -> p (t i)").bitcast(I32))
+
+        def load_w1(a, b):
+            for e in range(2):
+                c0 = b * PASS + e * half
+                nc.sync.dma_start(
+                    out=w1_raw[a, b, e][:],
+                    in_=w1[a * PASS:(a + 1) * PASS, c0:c0 + half].rearrange("(p j) c -> p j c", j=PACK))
+
+        def load_rows(tile, vec):
+            nc.sync.dma_start(out=tile[:].rearrange("p (b i) -> p b i", i=PACK),
+                              in_=vec.rearrange("(b p i) -> p b i", p=P, i=PACK))
+
+        def load_plane(queue, plane, scales):
+            for q in range(4):
+                queue.dma_start(
+                    out=plane[32 * q:32 * q + 4, :].bitcast(I32).rearrange("r (a c) -> r a c", a=HP),
+                    in_=scales[:, 4 * q:4 * q + 4, :].bitcast(I32).rearrange("a r c -> r a c"))
+
+        load_tab(0)
+        nc.sync.dma_start(offs_sb[:], offs)
+        load_w1(0, 0)
+        for q in range(4):
+            nc.sync.dma_start(out=tab_sc[32 * q:32 * q + 4 * KP, :].bitcast(I32),
+                              in_=tab_scales[:, 4 * q:4 * q + 4, :].bitcast(I32))
+        load_tab(1)
+        load_rows(temp_sb, temp)
+        load_w1(1, 0)
+        load_tab(2)
+        load_plane(nc.sync, w2_sc_raw, w2_scales)
+        load_w1(2, 0)
+        nc.sync.dma_start(pos1_sb[:], pos1)
+        nc.sync.dma_start(pos2_sb[:], pos2)
+        load_rows(lift_sb, lift)
+        for a in range(KP):
+            load_w1(a, 1)
+        care_v = care.rearrange("(b p i) j -> b p i j", p=P, i=PACK)
+        nc.sync.dma_start(out=care_sb[0][:], in_=care_v[0])
+        nc.sync.dma_start(out=w2_raw[:].bitcast(I32).rearrange("p (a c) -> p a c", a=HP),
+                          in_=w2_words.bitcast(I32).rearrange("a p c -> p a c"))
+        nc.sync.dma_start(out=w3_raw[:], in_=w3.rearrange("(p j) c -> p j c", j=PACK))
+        nc.sync.dma_start(out=w4_sb[:].bitcast(I32).rearrange("p (a c) -> p a c", a=HP),
+                          in_=w4_words.rearrange("a p c i -> a p (c i)").bitcast(I32).rearrange("a p c -> p a c"))
+        nc.sync.dma_start(out=care_sb[1][:], in_=care_v[1])
+
+        load_plane(nc.gpsimd, w4_sc, w4_scales)
+        nc.gpsimd.dma_start(out=bias_sb[:], in_=bias.rearrange("(p i) -> p i", i=PACK))
+        nc.gpsimd.dma_start(out=gain_sb[:], in_=gain.rearrange("(p i) -> p i", i=PACK))
+
+        def gather_tab(a):
+            nc.vector.tensor_copy(out=v_words[a][:], in_=tab_sb[a][:].indirect(offs_sb[:]))
+
+        w1_bf = {}
+
+        def round_w1(a, b, e, engine_copy):
+            if e == 0:
+                w1_bf[a, b] = work.tile([P, PASS * PACK], BF16, name="w1_bf", tag="w1_bf", align_bytes=64)
+            dst = w1_bf[a, b][:].rearrange("p (t m j) -> p m j t", t=PACK, j=PACK)
+            m0 = e * (half // PACK)
+            engine_copy(out=dst[:, m0:m0 + half // PACK],
+                        in_=w1_raw[a, b, e][:].rearrange("p j (m t) -> p m j t", t=PACK))
+
+        def quantize_w1(a, b):
+            nc.vector.quantize_mx(out=w1_words[a, b][:].bitcast(FP8X4), scales=w1_sc[a, b][:], in_=w1_bf[a, b][:])
+
+        for a in range(KP):
+            gather_tab(a)
+            if a == 0:
+                nc.vector.tensor_copy(out=v_sc[:], in_=tab_sc[:].indirect(offs_sb[:]))
+            round_w1(a, 0, 0, nc.scalar.copy)
+            round_w1(a, 0, 1, nc.vector.tensor_copy if a == KP - 1 else nc.scalar.copy)
+            if a == 0:
+                nc.scalar.mul(neg_temp[:], temp_sb[:], -1.0)
+            quantize_w1(a, 0)
+            if a == 1:
+                nc.vector.tensor_copy(out=w2_sc[:].rearrange("p (a t m) -> p a t m", a=HP, t=PACK),
+                                      in_=w2_sc_raw[:].rearrange("p (a m t) -> p a t m", a=HP, t=PACK))
+
+        state = {}
+
+        def product(i):
+            b, t = divmod(i, PACK)
+            banks = [psum.tile([P, BANK], F32, name="h_ps%d" % s, tag="h_ps%d" % s) for s in range(2)]
+            for a in range(KP):
+                for s in range(2):
+                    cols = slice(s * BANK, (s + 1) * BANK)
+                    nc.tensor.matmul_mx(
+                        out=banks[s][:],
+                        lhsT=w1_words[a, b][:, t * P:(t + 1) * P].bitcast(FP8X4),
+                        lhsT_scale=w1_sc[a, b][:, t * P:(t + 1) * P],
+                        rhs=v_words[a][:, cols].bitcast(FP8X4),
+                        rhs_scale=v_sc[4 * a:P, cols],
+                        start=(a == 0), stop=(a == KP - 1))
+            h = work.tile([P, S], F32, name="h", tag="h", bufs=3)
+            tops = work.tile([P, 2], F32, name="tops", tag="tops", bufs=3)
+            state[i] = dict(banks=banks, h=h, tops=tops)
+
+        def leave_bank(i, s):
+            st = state[i]
+            nc.vector.tensor_scalar(
+                out=st["h"][:, s * BANK:(s + 1) * BANK], in0=st["banks"][s][:], scalar1=1.0,
+                scalar2=None if s == 0 else st["tops"][:, 0:1],
+                op0=ALU.mult, op1=ALU.max, accum_out=st["tops"][:, s:s + 1])
+
+        def look(i, parts):
+            st = state[i]
+            shift = work.tile([P, 2], F32, name="shift", tag="shift", bufs=3)
+            nc.scalar.activation(out=shift[:, 0:1], in_=st["tops"][:, 1:2], func=ACT.Copy, scale=neg_temp[:, i:i + 1])
+            st["today"] = work.tile([P, J], F32, name="today", tag="today", bufs=3)
+            w = J // parts
+            for c in range(parts):
+                nc.scalar.activation(
+                    out=st["today"][:, c * w:(c + 1) * w],
+                    in_=st["h"][:].indirect(pos1_sb[:, c * w // 16:(c + 1) * w // 16]),
+                    func=ACT.Exp, bias=shift[:, 0:1], scale=temp_sb[:, i:i + 1])
+
+        def pick(i, j0, w):
+            st = state[i]
+            if j0 == 0:
+                st["last"] = work.tile([P, J], F32, name="last", tag="last")
+            nc.vector.tensor_copy(out=st["last"][:, j0:j0 + w],
+                                  in_=st["h"][:].indirect(pos2_sb[:, j0 // 16:(j0 + w) // 16]))
+
+        def take_larger(i, j0, w):
+            b, t = divmod(i, PACK)
+            st = state[i]
+            nc.vector.scalar_tensor_tensor(
+                out=larger[b][:, t, j0:j0 + w], in0=st["today"][:, j0:j0 + w], scalar=lift_sb[:, i:i + 1],
+                in1=st["last"][:, j0:j0 + w], op0=ALU.mult, op1=ALU.max)
+
+        def weigh(b, j0, w):
+            nc.vector.tensor_tensor(
+                out=worst_bf[b][:, j0 * PACK:(j0 + w) * PACK].rearrange("p (c x t) -> p c t x", x=4, t=PACK),
+                in0=larger[b][:, :, j0:j0 + w].rearrange("p t (c x) -> p c t x", x=4),
+                in1=care_sb[b][:, :, j0:j0 + w].rearrange("p t (c x) -> p c t x", x=4),
+                op=ALU.mult)
+
+        def quantize_worst(b, j0, w):
+            nc.vector.quantize_mx(out=worst_words[b][:, j0:j0 + w].bitcast(FP8X4), scales=worst_sc[b][:, j0:j0 + w],
+                                  in_=worst_bf[b][:, j0 * PACK:(j0 + w) * PACK])
+
+        last_tile = HP * PACK - 1
+        product(0)
+        for i in range(last_tile + 1):
+            if i < last_tile:
+                product(i + 1)
+            leave_bank(i, 0)
+            if i > 0:
+                pick(i - 1, 0, J)
+            leave_bank(i, 1)
+            look(i, 2 if i == last_tile else 1)
+            if i > 0:
+                take_larger(i - 1, 0, J)
+            if i < KP:
+                round_w1(i, 1, 0, nc.scalar.copy)
+                round_w1(i, 1, 1, nc.scalar.copy)
+            if 1 <= i <= KP - 1:
+                quantize_w1(i - 1, 1)
+            if i == KP - 1:
+                quantize_w1(i, 1)
+            if i == PACK:
+                nc.scalar.copy(out=w2_sb[:].bitcast(U16).rearrange("p (a t m) -> p a t m", a=HP, t=PACK),
+                               in_=w2_raw[:].bitcast(U16).rearrange("p (a m t) -> p a t m", a=HP, t=PACK))
+                weigh(0, 0, J // 2)
+            if i == PACK + 1:
+                nc.scalar.copy(out=w3_bf[:].rearrange("p (c x j) -> p c j x", x=4, j=PACK),
+                               in_=w3_raw[:].rearrange("p j (c x) -> p c j x", x=4))
+                weigh(0, J // 2, J // 2)
+            if i == PACK + 2:
+                quantize_worst(0, 0, J)
+                nc.vector.quantize_mx(out=w3_words[:].bitcast(FP8X4), scales=w3_sc[:], in_=w3_bf[:])
+
+        out_v = out.rearrange("(g p) j -> p g j", p=P)
+        chunk = {}
+
+        def front(c):
+            j0 = c * CH
+            cols = slice(j0, j0 + CH)
+            first = psum.tile([P, PACK, CH], F32, name="first", tag="first")
+            for t in range(PACK):
+                for a in range(HP):
+                    c0 = a * M + t * P
+                    nc.tensor.matmul_mx(
+                        out=first[:, t, :],
+                        lhsT=w2_sb[:, 2 * c0:2 * (c0 + P)].bitcast(FP4X4), lhsT_scale=w2_sc[:, c0:c0 + P],
+                        rhs=worst_words[a][:, cols].bitcast(FP8X4), rhs_scale=worst_sc[a][:, cols],
+                        start=(a == 0), stop=(a == HP - 1))
+            scores = psum.tile([P, NT, CH], F32, name="scores", tag="scores")
+            for g in range(NT):
+                for a in range(HP):
+                    c0 = a * N + g * P
+                    nc.tensor.matmul_mx(
+                        out=scores[:, g, :],
+                        lhsT=w4_sb[:, c0:c0 + P].bitcast(FP8X4), lhsT_scale=w4_sc[:, c0:c0 + P],
+                        rhs=worst_words[a][:, cols].bitcast(FP8X4), rhs_scale=worst_sc[a][:, cols],
+                        start=(a == 0 and g == 0), stop=False)
+            curve = work.tile([P, PACK, CH], F32, name="curve", tag="curve")
+            for t in range(PACK):
+                nc.scalar.activation(out=curve[:, t, :], in_=first[:, t, :], func=ACT.Tanh, bias=bias_sb[:, t:t + 1])
+            chunk[c] = dict(scores=scores, curve=curve)
+
+        def bend(c):
+            bent_bf = work.tile([P, CH * PACK], BF16, name="bent_bf", tag="bent_bf", align_bytes=64)
+            nc.vector.tensor_tensor(
+                out=bent_bf[:].rearrange("p (c x t) -> p c t x", x=4, t=PACK),
+                in0=chunk[c]["curve"][:].rearrange("p t (c x) -> p c t x", x=4),
+                in1=gain_sb[:].rearrange("p (c t x) -> p c t x", c=1, x=1).to_broadcast([P, CH // 4, PACK, 4]),
+                op=ALU.mult)
+            chunk[c]["bent_bf"] = bent_bf
+
+        def back(c):
+            bent_words = work.tile([P, CH], U32, name="bent_words", tag="bent_words", align_bytes=64)
+            bent_sc = work.tile([P, CH], U8, name="bent_sc", tag="bent_sc", align_bytes=64)
+            nc.vector.quantize_mx(out=bent_words[:].bitcast(FP8X4), scales=bent_sc[:], in_=chunk[c]["bent_bf"][:])
+            scores = chunk[c]["scores"]
+            for g in range(NT):
+                nc.tensor.matmul_mx(
+                    out=scores[:, g, :],
+                    lhsT=w3_words[:, g * P:(g + 1) * P].bitcast(FP8X4), lhsT_scale=w3_sc[:, g * P:(g + 1) * P],
+                    rhs=bent_words[:].bitcast(FP8X4), rhs_scale=bent_sc[:],
+                    start=False, stop=(g == NT - 1))
+            result = work.tile([P, NT, CH], F32, name="result", tag="result", bufs=4)
+            nc.scalar.copy(out=result[:], in_=scores[:])
+            nc.sync.dma_start(out=out_v[:, :, c * CH:(c + 1) * CH], in_=result[:])
+
+        chunks = J // CH
+        pick(last_tile, 0, CH)
+        for c in range(chunks + 2):
+            if c + 1 < chunks:
+                pick(last_tile, (c + 1) * CH, CH)
+            if c < chunks:
+                take_larger(last_tile, c * CH, CH)
+            if 2 <= c:
+                bend(c - 2)
+            if c < chunks:
+                weigh(1, c * CH, CH)
+            if 2 <= c:
+                back(c - 2)
+            if c < chunks:
+                quantize_worst(1, c * CH, CH)
+                front(c)

@@ -48,12 +48,7 @@ def tile_list_wound_dressing_scores_kernel(
         tab_sc = kept("tab_sc", [P, T], U8)
         v_words = [kept("v_words%d" % a, [P, S], U32) for a in range(KP)]
         v_sc = kept("v_sc", [P, S], U8)
-        half = PASS // 2
-        w1_raw = {}
-        for b in range(HP):
-            for a in range(KP):
-                for e in range(2):
-                    w1_raw[a, b, e] = kept("w1_raw%d%d%d" % (a, b, e), [P, PACK, half], F32)
+        w1_raw = {(a, b): kept("w1_raw%d%d" % (a, b), [P, PACK, PASS], F32) for a in range(KP) for b in range(HP)}
         w1_words = {(a, b): kept("w1_words%d%d" % (a, b), [P, PASS], U32) for a in range(KP) for b in range(HP)}
         w1_sc = {(a, b): kept("w1_sc%d%d" % (a, b), [P, PASS], U8) for a in range(KP) for b in range(HP)}
         temp_sb = kept("temp_sb", [P, HP * PACK], F32)
@@ -72,7 +67,7 @@ def tile_list_wound_dressing_scores_kernel(
         w3_bf = kept("w3_bf", [P, N * PACK], BF16)
         w3_words = kept("w3_words", [P, N], U32)
         w3_sc = kept("w3_sc", [P, N], U8)
-        larger = [kept("larger%d" % b, [P, PACK, J], F32) for b in range(HP)]
+        worst_rows = [kept("worst_rows%d" % b, [P, PACK, J], BF16) for b in range(HP)]
         worst_bf = [kept("worst_bf%d" % b, [P, J * PACK], BF16) for b in range(HP)]
         worst_words = [kept("worst_words%d" % b, [P, J], U32) for b in range(HP)]
         worst_sc = [kept("worst_sc%d" % b, [P, J], U8) for b in range(HP)]
@@ -85,11 +80,9 @@ def tile_list_wound_dressing_scores_kernel(
                               in_=tab_words[a].rearrange("p t i -> p (t i)").bitcast(I32))
 
         def load_w1(a, b):
-            for e in range(2):
-                c0 = b * PASS + e * half
-                nc.sync.dma_start(
-                    out=w1_raw[a, b, e][:],
-                    in_=w1[a * PASS:(a + 1) * PASS, c0:c0 + half].rearrange("(p j) c -> p j c", j=PACK))
+            nc.sync.dma_start(
+                out=w1_raw[a, b][:],
+                in_=w1[a * PASS:(a + 1) * PASS, b * PASS:(b + 1) * PASS].rearrange("(p j) c -> p j c", j=PACK))
 
         def load_rows(tile, vec):
             nc.sync.dma_start(out=tile[:].rearrange("p (b i) -> p b i", i=PACK),
@@ -103,62 +96,69 @@ def tile_list_wound_dressing_scores_kernel(
 
         load_tab(0)
         nc.sync.dma_start(offs_sb[:], offs)
-        load_w1(0, 0)
+        load_tab(1)
         for q in range(4):
             nc.sync.dma_start(out=tab_sc[32 * q:32 * q + 4 * KP, :].bitcast(I32),
                               in_=tab_scales[:, 4 * q:4 * q + 4, :].bitcast(I32))
-        load_tab(1)
+        load_w1(0, 0)
+        load_tab(2)
         load_rows(temp_sb, temp)
         load_w1(1, 0)
-        load_tab(2)
-        load_plane(nc.sync, w2_sc_raw, w2_scales)
         load_w1(2, 0)
         nc.sync.dma_start(pos1_sb[:], pos1)
         nc.sync.dma_start(pos2_sb[:], pos2)
         load_rows(lift_sb, lift)
-        for a in range(KP):
-            load_w1(a, 1)
         care_v = care.rearrange("(b p i) j -> b p i j", p=P, i=PACK)
+        load_w1(0, 1)
+        load_w1(1, 1)
         nc.sync.dma_start(out=care_sb[0][:], in_=care_v[0])
+        load_w1(2, 1)
         nc.sync.dma_start(out=w2_raw[:].bitcast(I32).rearrange("p (a c) -> p a c", a=HP),
                           in_=w2_words.bitcast(I32).rearrange("a p c -> p a c"))
-        nc.sync.dma_start(out=w3_raw[:], in_=w3.rearrange("(p j) c -> p j c", j=PACK))
+        load_plane(nc.sync, w2_sc_raw, w2_scales)
+        w3_v = w3.rearrange("(i t e) c -> t i e c", t=PACK, e=4)
+        for t in range(PACK):
+            nc.sync.dma_start(out=w3_raw[:, t, :], in_=w3_v[t])
         nc.sync.dma_start(out=w4_sb[:].bitcast(I32).rearrange("p (a c) -> p a c", a=HP),
                           in_=w4_words.rearrange("a p c i -> a p (c i)").bitcast(I32).rearrange("a p c -> p a c"))
         nc.sync.dma_start(out=care_sb[1][:], in_=care_v[1])
 
-        load_plane(nc.gpsimd, w4_sc, w4_scales)
-        nc.gpsimd.dma_start(out=bias_sb[:], in_=bias.rearrange("(p i) -> p i", i=PACK))
-        nc.gpsimd.dma_start(out=gain_sb[:], in_=gain.rearrange("(p i) -> p i", i=PACK))
+        load_plane(nc.sync, w4_sc, w4_scales)
+        with nc.allow_non_contiguous_dma(reason="512 values dealt four to a partition"):
+            for e in range(4):
+                nc.sync.dma_start(out=bias_sb[e:P:4, :], in_=bias.rearrange("(i t e) -> e i t", t=PACK, e=4)[e])
+                nc.sync.dma_start(out=gain_sb[e:P:4, :], in_=gain.rearrange("(i t e) -> e i t", t=PACK, e=4)[e])
 
         def gather_tab(a):
             nc.vector.tensor_copy(out=v_words[a][:], in_=tab_sb[a][:].indirect(offs_sb[:]))
 
         w1_bf = {}
 
-        def round_w1(a, b, e, engine_copy):
-            if e == 0:
+        def round_w1(a, b, u, engine_copy):
+            if u == 0:
                 w1_bf[a, b] = work.tile([P, PASS * PACK], BF16, name="w1_bf", tag="w1_bf", align_bytes=64)
-            dst = w1_bf[a, b][:].rearrange("p (t m j) -> p m j t", t=PACK, j=PACK)
-            m0 = e * (half // PACK)
-            engine_copy(out=dst[:, m0:m0 + half // PACK],
-                        in_=w1_raw[a, b, e][:].rearrange("p j (m t) -> p m j t", t=PACK))
+            engine_copy(out=w1_bf[a, b][:].rearrange("p (u e m j) -> p u m j e", u=2, e=2, j=PACK)[:, u],
+                        in_=w1_raw[a, b][:].rearrange("p j (m u e) -> p u m j e", u=2, e=2)[:, u])
 
-        def quantize_w1(a, b):
-            nc.vector.quantize_mx(out=w1_words[a, b][:].bitcast(FP8X4), scales=w1_sc[a, b][:], in_=w1_bf[a, b][:])
+        def quantize_w1(a, b, c0=0, w=PASS):
+            nc.vector.quantize_mx(out=w1_words[a, b][:, c0:c0 + w].bitcast(FP8X4), scales=w1_sc[a, b][:, c0:c0 + w],
+                                  in_=w1_bf[a, b][:, c0 * PACK:(c0 + w) * PACK])
 
-        for a in range(KP):
-            gather_tab(a)
-            if a == 0:
-                nc.vector.tensor_copy(out=v_sc[:], in_=tab_sc[:].indirect(offs_sb[:]))
-            round_w1(a, 0, 0, nc.scalar.copy)
-            round_w1(a, 0, 1, nc.vector.tensor_copy if a == KP - 1 else nc.scalar.copy)
-            if a == 0:
-                nc.scalar.mul(neg_temp[:], temp_sb[:], -1.0)
-            quantize_w1(a, 0)
-            if a == 1:
-                nc.vector.tensor_copy(out=w2_sc[:].rearrange("p (a t m) -> p a t m", a=HP, t=PACK),
-                                      in_=w2_sc_raw[:].rearrange("p (a m t) -> p a t m", a=HP, t=PACK))
+        gather_tab(0)
+        gather_tab(1)
+        nc.vector.tensor_copy(out=v_sc[:], in_=tab_sc[:].indirect(offs_sb[:]))
+        round_w1(0, 0, 0, nc.scalar.copy)
+        round_w1(0, 0, 1, nc.scalar.copy)
+        nc.scalar.mul(neg_temp[:], temp_sb[:], -1.0)
+        gather_tab(2)
+        quantize_w1(0, 0)
+        round_w1(1, 0, 0, nc.vector.tensor_copy)
+        round_w1(1, 0, 1, nc.scalar.copy)
+        quantize_w1(1, 0)
+        round_w1(2, 0, 0, nc.vector.tensor_copy)
+        round_w1(2, 0, 1, nc.scalar.copy)
+        quantize_w1(2, 0, 0, PASS // 2)
+        quantize_w1(2, 0, PASS // 2, PASS // 2)
 
         state = {}
 
@@ -206,18 +206,23 @@ def tile_list_wound_dressing_scores_kernel(
                                   in_=st["h"][:].indirect(pos2_sb[:, j0 // 16:(j0 + w) // 16]))
 
         def take_larger(i, j0, w):
-            b, t = divmod(i, PACK)
             st = state[i]
+            if j0 == 0:
+                st["larger"] = work.tile([P, J], F32, name="larger", tag="larger", bufs=3)
             nc.vector.scalar_tensor_tensor(
-                out=larger[b][:, t, j0:j0 + w], in0=st["today"][:, j0:j0 + w], scalar=lift_sb[:, i:i + 1],
+                out=st["larger"][:, j0:j0 + w], in0=st["today"][:, j0:j0 + w], scalar=lift_sb[:, i:i + 1],
                 in1=st["last"][:, j0:j0 + w], op0=ALU.mult, op1=ALU.max)
 
-        def weigh(b, j0, w):
+        def weigh(i, j0, w):
+            b, t = divmod(i, PACK)
             nc.vector.tensor_tensor(
+                out=worst_rows[b][:, t, j0:j0 + w], in0=state[i]["larger"][:, j0:j0 + w],
+                in1=care_sb[b][:, t, j0:j0 + w], op=ALU.mult)
+
+        def weave(b, j0, w, engine_copy):
+            engine_copy(
                 out=worst_bf[b][:, j0 * PACK:(j0 + w) * PACK].rearrange("p (c x t) -> p c t x", x=4, t=PACK),
-                in0=larger[b][:, :, j0:j0 + w].rearrange("p t (c x) -> p c t x", x=4),
-                in1=care_sb[b][:, :, j0:j0 + w].rearrange("p t (c x) -> p c t x", x=4),
-                op=ALU.mult)
+                in_=worst_rows[b][:, :, j0:j0 + w].rearrange("p t (c x) -> p c t x", x=4))
 
         def quantize_worst(b, j0, w):
             nc.vector.quantize_mx(out=worst_words[b][:, j0:j0 + w].bitcast(FP8X4), scales=worst_sc[b][:, j0:j0 + w],
@@ -226,11 +231,15 @@ def tile_list_wound_dressing_scores_kernel(
         last_tile = HP * PACK - 1
         product(0)
         for i in range(last_tile + 1):
-            if i < last_tile:
-                product(i + 1)
             leave_bank(i, 0)
             if i > 0:
                 pick(i - 1, 0, J)
+            if 1 <= i <= KP:
+                quantize_w1(i - 1, 1)
+            if i < last_tile:
+                product(i + 1)
+            if i > 1:
+                weigh(i - 2, 0, J)
             leave_bank(i, 1)
             look(i, 2 if i == last_tile else 1)
             if i > 0:
@@ -238,57 +247,60 @@ def tile_list_wound_dressing_scores_kernel(
             if i < KP:
                 round_w1(i, 1, 0, nc.scalar.copy)
                 round_w1(i, 1, 1, nc.scalar.copy)
-            if 1 <= i <= KP - 1:
-                quantize_w1(i - 1, 1)
-            if i == KP - 1:
-                quantize_w1(i, 1)
-            if i == PACK:
-                nc.scalar.copy(out=w2_sb[:].bitcast(U16).rearrange("p (a t m) -> p a t m", a=HP, t=PACK),
-                               in_=w2_raw[:].bitcast(U16).rearrange("p (a m t) -> p a t m", a=HP, t=PACK))
-                weigh(0, 0, J // 2)
             if i == PACK + 1:
+                nc.scalar.copy(out=w2_sb[:].bitcast(U32).rearrange("p (a t i w) -> p a t i w", a=HP, t=PACK, w=2),
+                               in_=w2_raw[:].bitcast(U32).rearrange("p (a i t w) -> p a t i w", a=HP, t=PACK, w=2))
+                nc.scalar.copy(out=w2_sc[:].bitcast(U32).rearrange("p (a t i) -> p a t i", a=HP, t=PACK),
+                               in_=w2_sc_raw[:].bitcast(U32).rearrange("p (a i t) -> p a t i", a=HP, t=PACK))
+            if i == PACK:
                 nc.scalar.copy(out=w3_bf[:].rearrange("p (c x j) -> p c j x", x=4, j=PACK),
                                in_=w3_raw[:].rearrange("p j (c x) -> p c j x", x=4))
-                weigh(0, J // 2, J // 2)
+            if i == PACK + 1:
+                nc.vector.quantize_mx(out=w3_words[:].bitcast(FP8X4), scales=w3_sc[:], in_=w3_bf[:])
+                weave(0, 0, J // 2, nc.scalar.copy)
+                weave(0, J // 2, J // 2, nc.scalar.copy)
             if i == PACK + 2:
                 quantize_worst(0, 0, J)
-                nc.vector.quantize_mx(out=w3_words[:].bitcast(FP8X4), scales=w3_sc[:], in_=w3_bf[:])
 
         out_v = out.rearrange("(g p) j -> p g j", p=P)
         chunk = {}
 
-        def front(c):
-            j0 = c * CH
-            cols = slice(j0, j0 + CH)
-            first = psum.tile([P, PACK, CH], F32, name="first", tag="first")
+        def passes(c, a):
+            cols = slice(c * CH, (c + 1) * CH)
+            if a == 0:
+                first = psum.tile([P, PACK, CH], F32, name="first", tag="first", bufs=J // CH)
+                chunk[c] = dict(first=first)
             for t in range(PACK):
-                for a in range(HP):
-                    c0 = a * M + t * P
-                    nc.tensor.matmul_mx(
-                        out=first[:, t, :],
-                        lhsT=w2_sb[:, 2 * c0:2 * (c0 + P)].bitcast(FP4X4), lhsT_scale=w2_sc[:, c0:c0 + P],
-                        rhs=worst_words[a][:, cols].bitcast(FP8X4), rhs_scale=worst_sc[a][:, cols],
-                        start=(a == 0), stop=(a == HP - 1))
-            scores = psum.tile([P, NT, CH], F32, name="scores", tag="scores")
+                c0 = a * M + t * P
+                nc.tensor.matmul_mx(
+                    out=chunk[c]["first"][:, t, :],
+                    lhsT=w2_sb[:, 2 * c0:2 * (c0 + P)].bitcast(FP4X4), lhsT_scale=w2_sc[:, c0:c0 + P],
+                    rhs=worst_words[a][:, cols].bitcast(FP8X4), rhs_scale=worst_sc[a][:, cols],
+                    start=(a == 0 and t == 0), stop=(a == HP - 1 and t == PACK - 1))
+            if a == 0:
+                chunk[c]["scores"] = psum.tile([P, NT, CH], F32, name="scores", tag="h_ps%d" % (c % 2))
             for g in range(NT):
-                for a in range(HP):
-                    c0 = a * N + g * P
-                    nc.tensor.matmul_mx(
-                        out=scores[:, g, :],
-                        lhsT=w4_sb[:, c0:c0 + P].bitcast(FP8X4), lhsT_scale=w4_sc[:, c0:c0 + P],
-                        rhs=worst_words[a][:, cols].bitcast(FP8X4), rhs_scale=worst_sc[a][:, cols],
-                        start=(a == 0 and g == 0), stop=False)
-            curve = work.tile([P, PACK, CH], F32, name="curve", tag="curve")
+                c0 = a * N + g * P
+                nc.tensor.matmul_mx(
+                    out=chunk[c]["scores"][:, g, :],
+                    lhsT=w4_sb[:, c0:c0 + P].bitcast(FP8X4), lhsT_scale=w4_sc[:, c0:c0 + P],
+                    rhs=worst_words[a][:, cols].bitcast(FP8X4), rhs_scale=worst_sc[a][:, cols],
+                    start=(a == 0 and g == 0), stop=False)
+
+        def front(c):
+            passes(c, 1)
+            curve = work.tile([P, PACK, CH], F32, name="curve", tag="curve", bufs=4)
             for t in range(PACK):
-                nc.scalar.activation(out=curve[:, t, :], in_=first[:, t, :], func=ACT.Tanh, bias=bias_sb[:, t:t + 1])
-            chunk[c] = dict(scores=scores, curve=curve)
+                nc.scalar.activation(out=curve[:, t, :], in_=chunk[c]["first"][:, t, :], func=ACT.Tanh,
+                                     bias=bias_sb[:, t:t + 1])
+            chunk[c]["curve"] = curve
 
         def bend(c):
             bent_bf = work.tile([P, CH * PACK], BF16, name="bent_bf", tag="bent_bf", align_bytes=64)
             nc.vector.tensor_tensor(
-                out=bent_bf[:].rearrange("p (c x t) -> p c t x", x=4, t=PACK),
-                in0=chunk[c]["curve"][:].rearrange("p t (c x) -> p c t x", x=4),
-                in1=gain_sb[:].rearrange("p (c t x) -> p c t x", c=1, x=1).to_broadcast([P, CH // 4, PACK, 4]),
+                out=bent_bf[:].rearrange("p (j t) -> p j t", t=PACK),
+                in0=chunk[c]["curve"][:].rearrange("p t j -> p j t"),
+                in1=gain_sb[:].rearrange("p (j t) -> p j t", j=1).to_broadcast([P, CH, PACK]),
                 op=ALU.mult)
             chunk[c]["bent_bf"] = bent_bf
 
@@ -308,18 +320,24 @@ def tile_list_wound_dressing_scores_kernel(
             nc.sync.dma_start(out=out_v[:, :, c * CH:(c + 1) * CH], in_=result[:])
 
         chunks = J // CH
+        for c in range(chunks):
+            passes(c, 0)
         pick(last_tile, 0, CH)
-        for c in range(chunks + 2):
+        weigh(last_tile - 1, 0, J)
+        for c in range(chunks):
+            take_larger(last_tile, c * CH, CH)
             if c + 1 < chunks:
                 pick(last_tile, (c + 1) * CH, CH)
-            if c < chunks:
-                take_larger(last_tile, c * CH, CH)
-            if 2 <= c:
-                bend(c - 2)
-            if c < chunks:
-                weigh(1, c * CH, CH)
-            if 2 <= c:
-                back(c - 2)
-            if c < chunks:
-                quantize_worst(1, c * CH, CH)
-                front(c)
+            if c > 0:
+                quantize_worst(1, (c - 1) * CH, CH)
+                front(c - 1)
+            weigh(last_tile, c * CH, CH)
+            if c + 1 == chunks:
+                bend(0)
+            weave(1, c * CH, CH, nc.scalar.copy if c + 1 < chunks else nc.vector.tensor_copy)
+        back(0)
+        quantize_worst(1, (chunks - 1) * CH, CH)
+        front(chunks - 1)
+        for c in range(1, chunks):
+            bend(c)
+            back(c)

@@ -72,7 +72,8 @@ def tile_list_wound_dressing_scores_kernel(
         worst_words = [kept("worst_words%d" % b, [P, J], U32) for b in range(HP)]
         worst_sc = [kept("worst_sc%d" % b, [P, J], U8) for b in range(HP)]
 
-        for plane in (tab_sc, w2_sc_raw, w4_sc):
+        nc.gpsimd.memset(tab_sc[:].bitcast(I32), 0)
+        for plane in (w2_sc_raw, w4_sc):
             nc.vector.memset(plane[:].bitcast(I32), 0)
 
         def load_tab(a):
@@ -101,9 +102,9 @@ def tile_list_wound_dressing_scores_kernel(
             nc.sync.dma_start(out=tab_sc[32 * q:32 * q + 4 * KP, :].bitcast(I32),
                               in_=tab_scales[:, 4 * q:4 * q + 4, :].bitcast(I32))
         load_w1(0, 0)
-        load_tab(2)
-        load_rows(temp_sb, temp)
         load_w1(1, 0)
+        load_rows(temp_sb, temp)
+        load_tab(2)
         load_w1(2, 0)
         nc.sync.dma_start(pos1_sb[:], pos1)
         nc.sync.dma_start(pos2_sb[:], pos2)
@@ -111,8 +112,8 @@ def tile_list_wound_dressing_scores_kernel(
         care_v = care.rearrange("(b p i) j -> b p i j", p=P, i=PACK)
         load_w1(0, 1)
         load_w1(1, 1)
-        nc.sync.dma_start(out=care_sb[0][:], in_=care_v[0])
         load_w1(2, 1)
+        nc.sync.dma_start(out=care_sb[0][:], in_=care_v[0])
         nc.sync.dma_start(out=w2_raw[:].bitcast(I32).rearrange("p (a c) -> p a c", a=HP),
                           in_=w2_words.bitcast(I32).rearrange("a p c -> p a c"))
         load_plane(nc.sync, w2_sc_raw, w2_scales)
@@ -149,12 +150,12 @@ def tile_list_wound_dressing_scores_kernel(
         nc.vector.tensor_copy(out=v_sc[:], in_=tab_sc[:].indirect(offs_sb[:]))
         round_w1(0, 0, 0, nc.scalar.copy)
         round_w1(0, 0, 1, nc.scalar.copy)
-        nc.scalar.mul(neg_temp[:], temp_sb[:], -1.0)
-        gather_tab(2)
         quantize_w1(0, 0)
         round_w1(1, 0, 0, nc.vector.tensor_copy)
         round_w1(1, 0, 1, nc.scalar.copy)
+        nc.scalar.mul(neg_temp[:], temp_sb[:], -1.0)
         quantize_w1(1, 0)
+        gather_tab(2)
         round_w1(2, 0, 0, nc.vector.tensor_copy)
         round_w1(2, 0, 1, nc.scalar.copy)
         quantize_w1(2, 0, 0, PASS // 2)
@@ -208,14 +209,14 @@ def tile_list_wound_dressing_scores_kernel(
         def take_larger(i, j0, w):
             st = state[i]
             if j0 == 0:
-                st["larger"] = work.tile([P, J], F32, name="larger", tag="larger", bufs=3)
+                st["larger"] = work.tile([P, J], F32, name="larger", tag="larger", bufs=4)
             nc.vector.scalar_tensor_tensor(
                 out=st["larger"][:, j0:j0 + w], in0=st["today"][:, j0:j0 + w], scalar=lift_sb[:, i:i + 1],
                 in1=st["last"][:, j0:j0 + w], op0=ALU.mult, op1=ALU.max)
 
-        def weigh(i, j0, w):
+        def weigh(i, j0, w, engine):
             b, t = divmod(i, PACK)
-            nc.vector.tensor_tensor(
+            engine.tensor_tensor(
                 out=worst_rows[b][:, t, j0:j0 + w], in0=state[i]["larger"][:, j0:j0 + w],
                 in1=care_sb[b][:, t, j0:j0 + w], op=ALU.mult)
 
@@ -238,27 +239,27 @@ def tile_list_wound_dressing_scores_kernel(
                 quantize_w1(i - 1, 1)
             if i < last_tile:
                 product(i + 1)
-            if i > 1:
-                weigh(i - 2, 0, J)
             leave_bank(i, 1)
             look(i, 2 if i == last_tile else 1)
             if i > 0:
                 take_larger(i - 1, 0, J)
+                weigh(i - 1, 0, J, nc.gpsimd)
             if i < KP:
                 round_w1(i, 1, 0, nc.scalar.copy)
                 round_w1(i, 1, 1, nc.scalar.copy)
-            if i == PACK + 1:
+            if i == PACK - 1:
                 nc.scalar.copy(out=w2_sb[:].bitcast(U32).rearrange("p (a t i w) -> p a t i w", a=HP, t=PACK, w=2),
                                in_=w2_raw[:].bitcast(U32).rearrange("p (a i t w) -> p a t i w", a=HP, t=PACK, w=2))
                 nc.scalar.copy(out=w2_sc[:].bitcast(U32).rearrange("p (a t i) -> p a t i", a=HP, t=PACK),
                                in_=w2_sc_raw[:].bitcast(U32).rearrange("p (a i t) -> p a t i", a=HP, t=PACK))
-            if i == PACK:
-                nc.scalar.copy(out=w3_bf[:].rearrange("p (c x j) -> p c j x", x=4, j=PACK),
-                               in_=w3_raw[:].rearrange("p j (c x) -> p c j x", x=4))
+            if i in (PACK - 1, PACK):
+                c0 = (i - PACK + 1) * (N // 8)
+                nc.scalar.copy(out=w3_bf[:].rearrange("p (c x j) -> p c j x", x=4, j=PACK)[:, c0:c0 + N // 8],
+                               in_=w3_raw[:].rearrange("p j (c x) -> p c j x", x=4)[:, c0:c0 + N // 8])
+            if i in (PACK, PACK + 1):
+                weave(0, (i - PACK) * (J // 2), J // 2, nc.scalar.copy)
             if i == PACK + 1:
                 nc.vector.quantize_mx(out=w3_words[:].bitcast(FP8X4), scales=w3_sc[:], in_=w3_bf[:])
-                weave(0, 0, J // 2, nc.scalar.copy)
-                weave(0, J // 2, J // 2, nc.scalar.copy)
             if i == PACK + 2:
                 quantize_worst(0, 0, J)
 
@@ -322,22 +323,22 @@ def tile_list_wound_dressing_scores_kernel(
         chunks = J // CH
         for c in range(chunks):
             passes(c, 0)
-        pick(last_tile, 0, CH)
-        weigh(last_tile - 1, 0, J)
-        for c in range(chunks):
-            take_larger(last_tile, c * CH, CH)
-            if c + 1 < chunks:
-                pick(last_tile, (c + 1) * CH, CH)
-            if c > 0:
-                quantize_worst(1, (c - 1) * CH, CH)
-                front(c - 1)
-            weigh(last_tile, c * CH, CH)
-            if c + 1 == chunks:
-                bend(0)
-            weave(1, c * CH, CH, nc.scalar.copy if c + 1 < chunks else nc.vector.tensor_copy)
-        back(0)
-        quantize_worst(1, (chunks - 1) * CH, CH)
-        front(chunks - 1)
+        pick(last_tile, 0, J // 2)
+        take_larger(last_tile, 0, J // 2)
+        weigh(last_tile, 0, J // 2, nc.vector)
+        weave(1, 0, CH, nc.scalar.copy)
+        weave(1, CH, CH, nc.scalar.copy)
+        pick(last_tile, J // 2, J // 2)
+        take_larger(last_tile, J // 2, J // 2)
+        quantize_worst(1, 0, CH)
+        front(0)
+        weigh(last_tile, J // 2, J // 2, nc.vector)
+        weave(1, 2 * CH, 2 * CH, nc.vector.tensor_copy)
         for c in range(1, chunks):
-            bend(c)
-            back(c)
+            quantize_worst(1, c * CH, CH)
+            front(c)
+        for c in range(chunks + 1):
+            if c < chunks:
+                bend(c)
+            if c > 0:
+                back(c - 1)

@@ -56,7 +56,8 @@ def tile_list_wound_dressing_scores_kernel(
         lift_sb = kept("lift_sb", [P, HP * PACK], F32)
         bias_sb = kept("bias_sb", [P, PACK], F32)
         gain_sb = kept("gain_sb", [P, PACK], F32)
-        care_sb = [kept("care%d" % b, [P, PACK, J], F32) for b in range(HP)]
+        care_parts = [kept("care_a", [P, 1, J], F32), kept("care_b", [P, PACK - 1, J], F32), kept("care_c", [P, PACK, J], F32)]
+        care_rows = [part[:, t, :] for part in care_parts for t in range(part.shape[1])]
         w2_raw = kept("w2_raw", [P, HP * 2 * M], U8)
         w2_sb = kept("w2_sb", [P, HP * 2 * M], U8)
         w2_sc_raw = kept("w2_sc_raw", [P, HP * M], U8)
@@ -112,8 +113,9 @@ def tile_list_wound_dressing_scores_kernel(
         care_v = care.rearrange("(b p i) j -> b p i j", p=P, i=PACK)
         load_w1(0, 1)
         load_w1(1, 1)
+        nc.sync.dma_start(out=care_parts[0][:], in_=care_v[0][:, 0:1, :])
         load_w1(2, 1)
-        nc.sync.dma_start(out=care_sb[0][:], in_=care_v[0])
+        nc.sync.dma_start(out=care_parts[1][:], in_=care_v[0][:, 1:PACK, :])
         nc.sync.dma_start(out=w2_raw[:].bitcast(I32).rearrange("p (a c) -> p a c", a=HP),
                           in_=w2_words.bitcast(I32).rearrange("a p c -> p a c"))
         load_plane(nc.sync, w2_sc_raw, w2_scales)
@@ -122,7 +124,7 @@ def tile_list_wound_dressing_scores_kernel(
             nc.sync.dma_start(out=w3_raw[:, t, :], in_=w3_v[t])
         nc.sync.dma_start(out=w4_sb[:].bitcast(I32).rearrange("p (a c) -> p a c", a=HP),
                           in_=w4_words.rearrange("a p c i -> a p (c i)").bitcast(I32).rearrange("a p c -> p a c"))
-        nc.sync.dma_start(out=care_sb[1][:], in_=care_v[1])
+        nc.sync.dma_start(out=care_parts[2][:], in_=care_v[1])
 
         load_plane(nc.sync, w4_sc, w4_scales)
         with nc.allow_non_contiguous_dma(reason="512 values dealt four to a partition"):
@@ -184,13 +186,14 @@ def tile_list_wound_dressing_scores_kernel(
             st = state[i]
             nc.vector.tensor_scalar(
                 out=st["h"][:, s * BANK:(s + 1) * BANK], in0=st["banks"][s][:], scalar1=1.0,
-                scalar2=None if s == 0 else st["tops"][:, 0:1],
+                scalar2=None,
                 op0=ALU.mult, op1=ALU.max, accum_out=st["tops"][:, s:s + 1])
 
         def look(i, parts):
             st = state[i]
             shift = work.tile([P, 2], F32, name="shift", tag="shift", bufs=3)
-            nc.scalar.activation(out=shift[:, 0:1], in_=st["tops"][:, 1:2], func=ACT.Copy, scale=neg_temp[:, i:i + 1])
+            nc.vector.tensor_scalar(out=shift[:, 0:1], in0=st["tops"][:, 0:1], scalar1=st["tops"][:, 1:2],
+                                    scalar2=neg_temp[:, i:i + 1], op0=ALU.max, op1=ALU.mult)
             st["today"] = work.tile([P, J], F32, name="today", tag="today", bufs=3)
             w = J // parts
             for c in range(parts):
@@ -218,7 +221,7 @@ def tile_list_wound_dressing_scores_kernel(
             b, t = divmod(i, PACK)
             engine.tensor_tensor(
                 out=worst_rows[b][:, t, j0:j0 + w], in0=state[i]["larger"][:, j0:j0 + w],
-                in1=care_sb[b][:, t, j0:j0 + w], op=ALU.mult)
+                in1=care_rows[i][:, j0:j0 + w], op=ALU.mult)
 
         def weave(b, j0, w, engine_copy):
             engine_copy(
@@ -232,18 +235,18 @@ def tile_list_wound_dressing_scores_kernel(
         last_tile = HP * PACK - 1
         product(0)
         for i in range(last_tile + 1):
+            if i > 1:
+                take_larger(i - 2, 0, J)
+                weigh(i - 2, 0, J, nc.gpsimd)
             leave_bank(i, 0)
+            leave_bank(i, 1)
             if i > 0:
                 pick(i - 1, 0, J)
+            look(i, 2 if i == last_tile else 1)
             if 1 <= i <= KP:
                 quantize_w1(i - 1, 1)
             if i < last_tile:
                 product(i + 1)
-            leave_bank(i, 1)
-            look(i, 2 if i == last_tile else 1)
-            if i > 0:
-                take_larger(i - 1, 0, J)
-                weigh(i - 1, 0, J, nc.gpsimd)
             if i < KP:
                 round_w1(i, 1, 0, nc.scalar.copy)
                 round_w1(i, 1, 1, nc.scalar.copy)
@@ -256,10 +259,10 @@ def tile_list_wound_dressing_scores_kernel(
                 c0 = (i - PACK + 1) * (N // 8)
                 nc.scalar.copy(out=w3_bf[:].rearrange("p (c x j) -> p c j x", x=4, j=PACK)[:, c0:c0 + N // 8],
                                in_=w3_raw[:].rearrange("p j (c x) -> p c j x", x=4)[:, c0:c0 + N // 8])
-            if i in (PACK, PACK + 1):
-                weave(0, (i - PACK) * (J // 2), J // 2, nc.scalar.copy)
             if i == PACK + 1:
                 nc.vector.quantize_mx(out=w3_words[:].bitcast(FP8X4), scales=w3_sc[:], in_=w3_bf[:])
+                weave(0, 0, J // 2, nc.scalar.copy)
+                weave(0, J // 2, J // 2, nc.scalar.copy)
             if i == PACK + 2:
                 quantize_worst(0, 0, J)
 
@@ -323,12 +326,14 @@ def tile_list_wound_dressing_scores_kernel(
         chunks = J // CH
         for c in range(chunks):
             passes(c, 0)
+        take_larger(last_tile - 1, 0, J)
         pick(last_tile, 0, J // 2)
+        weigh(last_tile - 1, 0, J, nc.vector)
         take_larger(last_tile, 0, J // 2)
+        pick(last_tile, J // 2, J // 2)
         weigh(last_tile, 0, J // 2, nc.vector)
         weave(1, 0, CH, nc.scalar.copy)
         weave(1, CH, CH, nc.scalar.copy)
-        pick(last_tile, J // 2, J // 2)
         take_larger(last_tile, J // 2, J // 2)
         quantize_worst(1, 0, CH)
         front(0)

from contextlib import ExitStack

import concourse.mybir as mybir

K, H, M, N, T, S, J = 1536, 1024, 512, 384, 2048, 1024, 512
FLOPS = 2 * (K * H * S + H * M * J + M * N * J + H * N * J)

F32 = mybir.dt.float32
BF16 = mybir.dt.bfloat16
I32 = mybir.dt.int32
U32 = mybir.dt.uint32
U16 = mybir.dt.uint16
U8 = mybir.dt.uint8
FP8X4 = mybir.dt.float8_e4m3fn_x4
FP4X4 = mybir.dt.float4_e2m1fn_x4
ALU = mybir.AluOpType
ACT = mybir.ActivationFunctionType

P = 128
PACK = 4
PASS = P * PACK
KP = K // PASS
HP = H // PASS
BANK = 512
CH = 128
NT = N // P


def tile_list_wound_dressing_scores_kernel(
    tc, tab_words, tab_scales, offs, pos1, pos2, w1, temp, lift, care,
    w2_words, w2_scales, bias, gain, w3, w4_words, w4_scales, out,
):
    nc = tc.nc
    with ExitStack() as ctx:
        lists = ctx.enter_context(tc.tile_pool(name="lists", bufs=1))
        keep = ctx.enter_context(tc.tile_pool(name="keep", bufs=1))
        work = ctx.enter_context(tc.tile_pool(name="work", bufs=2))
        psum = ctx.enter_context(tc.psum_pool(name="psum", bufs=2))

        def kept(name, shape, dtype):
            return keep.tile(shape, dtype, name=name, align_bytes=64)

        offs_sb = lists.tile([P, S // 16], U16, name="offs_sb")
        pos1_sb = lists.tile([P, J // 16], U16, name="pos1_sb")
        pos2_sb = lists.tile([P, J // 16], U16, name="pos2_sb")

        tab_sb = [kept("tab%d" % a, [P, T], U32) for a in range(KP)]
        tab_sc = kept("tab_sc", [P, T], U8)
        v_words = [kept("v_words%d" % a, [P, S], U32) for a in range(KP)]
        v_sc = kept("v_sc", [P, S], U8)
        w1_raw = {(a, b): kept("w1_raw%d%d" % (a, b), [P, PACK, PASS], F32) for a in range(KP) for b in range(HP)}
        w1_words = {(a, b): kept("w1_words%d%d" % (a, b), [P, PASS], U32) for a in range(KP) for b in range(HP)}
        w1_sc = {(a, b): kept("w1_sc%d%d" % (a, b), [P, PASS], U8) for a in range(KP) for b in range(HP)}
        temp_sb = kept("temp_sb", [P, HP * PACK], F32)
        neg_temp = kept("neg_temp", [P, HP * PACK], F32)
        lift_sb = kept("lift_sb", [P, HP * PACK], F32)
        bias_sb = kept("bias_sb", [P, PACK], F32)
        gain_sb = kept("gain_sb", [P, PACK], F32)
        care_parts = [kept("care_a", [P, 1, J], F32), kept("care_b", [P, PACK - 1, J], F32), kept("care_c", [P, PACK, J], F32)]
        care_rows = [part[:, t, :] for part in care_parts for t in range(part.shape[1])]
        w2_raw = kept("w2_raw", [P, HP * 2 * M], U8)
        w2_sb = kept("w2_sb", [P, HP * 2 * M], U8)
        w2_sc_raw = kept("w2_sc_raw", [P, HP * M], U8)
        w2_sc = kept("w2_sc", [P, HP * M], U8)
        w4_sb = kept("w4_sb", [P, HP * N], U32)
        w4_sc = kept("w4_sc", [P, HP * N], U8)
        w3_raw = kept("w3_raw", [P, PACK, N], F32)
        w3_bf = kept("w3_bf", [P, N * PACK], BF16)
        w3_words = kept("w3_words", [P, N], U32)
        w3_sc = kept("w3_sc", [P, N], U8)
        worst_rows = [kept("worst_rows%d" % b, [P, PACK, J], BF16) for b in range(HP)]
        worst_bf = [kept("worst_bf%d" % b, [P, J * PACK], BF16) for b in range(HP)]
        worst_words = [kept("worst_words%d" % b, [P, J], U32) for b in range(HP)]
        worst_sc = [kept("worst_sc%d" % b, [P, J], U8) for b in range(HP)]

        nc.gpsimd.memset(tab_sc[:].bitcast(I32), 0)
        for plane in (w2_sc_raw, w4_sc):
            nc.vector.memset(plane[:].bitcast(I32), 0)

        def load_tab(a):
            nc.sync.dma_start(out=tab_sb[a][:].bitcast(I32),
                              in_=tab_words[a].rearrange("p t i -> p (t i)").bitcast(I32))

        def load_w1(a, b):
            nc.sync.dma_start(
                out=w1_raw[a, b][:],
                in_=w1[a * PASS:(a + 1) * PASS, b * PASS:(b + 1) * PASS].rearrange("(p j) c -> p j c", j=PACK))

        def load_rows(tile, vec):
            nc.sync.dma_start(out=tile[:].rearrange("p (b i) -> p b i", i=PACK),
                              in_=vec.rearrange("(b p i) -> p b i", p=P, i=PACK))

        def load_plane(queue, plane, scales):
            for q in range(4):
                queue.dma_start(
                    out=plane[32 * q:32 * q + 4, :].bitcast(I32).rearrange("r (a c) -> r a c", a=HP),
                    in_=scales[:, 4 * q:4 * q + 4, :].bitcast(I32).rearrange("a r c -> r a c"))

        load_tab(0)
        nc.sync.dma_start(offs_sb[:], offs)
        load_tab(1)
        for q in range(4):
            nc.sync.dma_start(out=tab_sc[32 * q:32 * q + 4 * KP, :].bitcast(I32),
                              in_=tab_scales[:, 4 * q:4 * q + 4, :].bitcast(I32))
        load_w1(0, 0)
        load_w1(1, 0)
        load_rows(temp_sb, temp)
        load_tab(2)
        load_w1(2, 0)
        nc.sync.dma_start(pos1_sb[:], pos1)
        nc.sync.dma_start(pos2_sb[:], pos2)
        load_rows(lift_sb, lift)
        care_v = care.rearrange("(b p i) j -> b p i j", p=P, i=PACK)
        load_w1(0, 1)
        load_w1(1, 1)
        nc.sync.dma_start(out=care_parts[0][:], in_=care_v[0][:, 0:1, :])
        load_w1(2, 1)
        nc.sync.dma_start(out=care_parts[1][:], in_=care_v[0][:, 1:PACK, :])
        nc.sync.dma_start(out=w2_raw[:].bitcast(I32).rearrange("p (a c) -> p a c", a=HP),
                          in_=w2_words.bitcast(I32).rearrange("a p c -> p a c"))
        load_plane(nc.sync, w2_sc_raw, w2_scales)
        w3_v = w3.rearrange("(i t e) c -> t i e c", t=PACK, e=4)
        for t in range(PACK):
            nc.sync.dma_start(out=w3_raw[:, t, :], in_=w3_v[t])
        nc.sync.dma_start(out=w4_sb[:].bitcast(I32).rearrange("p (a c) -> p a c", a=HP),
                          in_=w4_words.rearrange("a p c i -> a p (c i)").bitcast(I32).rearrange("a p c -> p a c"))
        nc.sync.dma_start(out=care_parts[2][:], in_=care_v[1])

        load_plane(nc.sync, w4_sc, w4_scales)
        with nc.allow_non_contiguous_dma(reason="512 values dealt four to a partition"):
            for e in range(4):
                nc.sync.dma_start(out=bias_sb[e:P:4, :], in_=bias.rearrange("(i t e) -> e i t", t=PACK, e=4)[e])
                nc.sync.dma_start(out=gain_sb[e:P:4, :], in_=gain.rearrange("(i t e) -> e i t", t=PACK, e=4)[e])

        def gather_tab(a):
            nc.vector.tensor_copy(out=v_words[a][:], in_=tab_sb[a][:].indirect(offs_sb[:]))

        w1_bf = {}

        def round_w1(a, b, u, engine_copy):
            if u == 0:
                w1_bf[a, b] = work.tile([P, PASS * PACK], BF16, name="w1_bf", tag="w1_bf", align_bytes=64)
            engine_copy(out=w1_bf[a, b][:].rearrange("p (u e m j) -> p u m j e", u=2, e=2, j=PACK)[:, u],
                        in_=w1_raw[a, b][:].rearrange("p j (m u e) -> p u m j e", u=2, e=2)[:, u])

        def quantize_w1(a, b, c0=0, w=PASS):
            nc.vector.quantize_mx(out=w1_words[a, b][:, c0:c0 + w].bitcast(FP8X4), scales=w1_sc[a, b][:, c0:c0 + w],
                                  in_=w1_bf[a, b][:, c0 * PACK:(c0 + w) * PACK])

        gather_tab(0)
        gather_tab(1)
        nc.vector.tensor_copy(out=v_sc[:], in_=tab_sc[:].indirect(offs_sb[:]))
        round_w1(0, 0, 0, nc.scalar.copy)
        round_w1(0, 0, 1, nc.scalar.copy)
        quantize_w1(0, 0)
        round_w1(1, 0, 0, nc.vector.tensor_copy)
        round_w1(1, 0, 1, nc.scalar.copy)
        nc.scalar.mul(neg_temp[:], temp_sb[:], -1.0)
        quantize_w1(1, 0)
        gather_tab(2)
        round_w1(2, 0, 0, nc.vector.tensor_copy)
        round_w1(2, 0, 1, nc.scalar.copy)
        quantize_w1(2, 0, 0, PASS // 2)
        quantize_w1(2, 0, PASS // 2, PASS // 2)

        state = {}

        def product(i):
            b, t = divmod(i, PACK)
            banks = [psum.tile([P, BANK], F32, name="h_ps%d" % s, tag="h_ps%d" % s) for s in range(2)]
            for a in range(KP):
                for s in range(2):
                    cols = slice(s * BANK, (s + 1) * BANK)
                    nc.tensor.matmul_mx(
                        out=banks[s][:],
                        lhsT=w1_words[a, b][:, t * P:(t + 1) * P].bitcast(FP8X4),
                        lhsT_scale=w1_sc[a, b][:, t * P:(t + 1) * P],
                        rhs=v_words[a][:, cols].bitcast(FP8X4),
                        rhs_scale=v_sc[4 * a:P, cols],
                        start=(a == 0), stop=(a == KP - 1))
            h = work.tile([P, S], F32, name="h", tag="h", bufs=3)
            tops = work.tile([P, 2], F32, name="tops", tag="tops", bufs=3)
            state[i] = dict(banks=banks, h=h, tops=tops)

        def leave_bank(i, s):
            st = state[i]
            nc.vector.tensor_scalar(
                out=st["h"][:, s * BANK:(s + 1) * BANK], in0=st["banks"][s][:], scalar1=1.0,
                scalar2=None,
                op0=ALU.mult, op1=ALU.max, accum_out=st["tops"][:, s:s + 1])

        def look(i, parts):
            st = state[i]
            shift = work.tile([P, 2], F32, name="shift", tag="shift", bufs=3)
            nc.vector.tensor_scalar(out=shift[:, 0:1], in0=st["tops"][:, 0:1], scalar1=st["tops"][:, 1:2],
                                    scalar2=neg_temp[:, i:i + 1], op0=ALU.max, op1=ALU.mult)
            st["today"] = work.tile([P, J], F32, name="today", tag="today", bufs=3)
            w = J // parts
            for c in range(parts):
                nc.scalar.activation(
                    out=st["today"][:, c * w:(c + 1) * w],
                    in_=st["h"][:].indirect(pos1_sb[:, c * w // 16:(c + 1) * w // 16]),
                    func=ACT.Exp, bias=shift[:, 0:1], scale=temp_sb[:, i:i + 1])

        def pick(i, j0, w):
            st = state[i]
            if j0 == 0:
                st["last"] = work.tile([P, J], F32, name="last", tag="last")
            nc.vector.tensor_copy(out=st["last"][:, j0:j0 + w],
                                  in_=st["h"][:].indirect(pos2_sb[:, j0 // 16:(j0 + w) // 16]))

        def take_larger(i, j0, w):
            st = state[i]
            if j0 == 0:
                st["larger"] = work.tile([P, J], F32, name="larger", tag="larger", bufs=4)
            nc.vector.scalar_tensor_tensor(
                out=st["larger"][:, j0:j0 + w], in0=st["today"][:, j0:j0 + w], scalar=lift_sb[:, i:i + 1],
                in1=st["last"][:, j0:j0 + w], op0=ALU.mult, op1=ALU.max)

        def weigh(i, j0, w, engine):
            b, t = divmod(i, PACK)
            engine.tensor_tensor(
                out=worst_rows[b][:, t, j0:j0 + w], in0=state[i]["larger"][:, j0:j0 + w],
                in1=care_rows[i][:, j0:j0 + w], op=ALU.mult)

        def weave(b, j0, w, engine_copy):
            engine_copy(
                out=worst_bf[b][:, j0 * PACK:(j0 + w) * PACK].rearrange("p (c x t) -> p c t x", x=4, t=PACK),
                in_=worst_rows[b][:, :, j0:j0 + w].rearrange("p t (c x) -> p c t x", x=4))

        def quantize_worst(b, j0, w):
            nc.vector.quantize_mx(out=worst_words[b][:, j0:j0 + w].bitcast(FP8X4), scales=worst_sc[b][:, j0:j0 + w],
                                  in_=worst_bf[b][:, j0 * PACK:(j0 + w) * PACK])

        last_tile = HP * PACK - 1
        product(0)
        for i in range(last_tile + 1):
            if i > 1:
                take_larger(i - 2, 0, J)
                weigh(i - 2, 0, J, nc.gpsimd)
            leave_bank(i, 0)
            leave_bank(i, 1)
            if i > 0:
                pick(i - 1, 0, J)
            look(i, 2 if i == last_tile else 1)
            if 1 <= i <= KP:
                quantize_w1(i - 1, 1)
            if i < last_tile:
                product(i + 1)
            if i < KP:
                round_w1(i, 1, 0, nc.scalar.copy)
                round_w1(i, 1, 1, nc.scalar.copy)
            if i == PACK - 1:
                nc.scalar.copy(out=w2_sb[:].bitcast(U32).rearrange("p (a t i w) -> p a t i w", a=HP, t=PACK, w=2),
                               in_=w2_raw[:].bitcast(U32).rearrange("p (a i t w) -> p a t i w", a=HP, t=PACK, w=2))
                nc.scalar.copy(out=w2_sc[:].bitcast(U32).rearrange("p (a t i) -> p a t i", a=HP, t=PACK),
                               in_=w2_sc_raw[:].bitcast(U32).rearrange("p (a i t) -> p a t i", a=HP, t=PACK))
            if i in (PACK - 1, PACK):
                c0 = (i - PACK + 1) * (N // 8)
                nc.scalar.copy(out=w3_bf[:].rearrange("p (c x j) -> p c j x", x=4, j=PACK)[:, c0:c0 + N // 8],
                               in_=w3_raw[:].rearrange("p j (c x) -> p c j x", x=4)[:, c0:c0 + N // 8])
            if i == PACK + 1:
                nc.vector.quantize_mx(out=w3_words[:].bitcast(FP8X4), scales=w3_sc[:], in_=w3_bf[:])
                weave(0, 0, J // 2, nc.scalar.copy)
                weave(0, J // 2, J // 2, nc.scalar.copy)
            if i == PACK + 2:
                quantize_worst(0, 0, J)

        out_v = out.rearrange("(g p) j -> p g j", p=P)
        chunk = {}

        def passes(c, a):
            cols = slice(c * CH, (c + 1) * CH)
            if a == 0:
                first = psum.tile([P, PACK, CH], F32, name="first", tag="first", bufs=J // CH)
                chunk[c] = dict(first=first)
            for t in range(PACK):
                c0 = a * M + t * P
                nc.tensor.matmul_mx(
                    out=chunk[c]["first"][:, t, :],
                    lhsT=w2_sb[:, 2 * c0:2 * (c0 + P)].bitcast(FP4X4), lhsT_scale=w2_sc[:, c0:c0 + P],
                    rhs=worst_words[a][:, cols].bitcast(FP8X4), rhs_scale=worst_sc[a][:, cols],
                    start=(a == 0 and t == 0), stop=(a == HP - 1 and t == PACK - 1))
            if a == 0:
                chunk[c]["scores"] = psum.tile([P, NT, CH], F32, name="scores", tag="h_ps%d" % (c % 2))
            for g in range(NT):
                c0 = a * N + g * P
                nc.tensor.matmul_mx(
                    out=chunk[c]["scores"][:, g, :],
                    lhsT=w4_sb[:, c0:c0 + P].bitcast(FP8X4), lhsT_scale=w4_sc[:, c0:c0 + P],
                    rhs=worst_words[a][:, cols].bitcast(FP8X4), rhs_scale=worst_sc[a][:, cols],
                    start=(a == 0 and g == 0), stop=False)

        def front(c):
            passes(c, 1)
            curve = work.tile([P, PACK, CH], F32, name="curve", tag="curve", bufs=4)
            for t in range(PACK):
                nc.scalar.activation(out=curve[:, t, :], in_=chunk[c]["first"][:, t, :], func=ACT.Tanh,
                                     bias=bias_sb[:, t:t + 1])
            chunk[c]["curve"] = curve

        def bend(c):
            bent_bf = work.tile([P, CH * PACK], BF16, name="bent_bf", tag="bent_bf", align_bytes=64)
            nc.vector.tensor_tensor(
                out=bent_bf[:].rearrange("p (j t) -> p j t", t=PACK),
                in0=chunk[c]["curve"][:].rearrange("p t j -> p j t"),
                in1=gain_sb[:].rearrange("p (j t) -> p j t", j=1).to_broadcast([P, CH, PACK]),
                op=ALU.mult)
            chunk[c]["bent_bf"] = bent_bf

        def back(c):
            bent_words = work.tile([P, CH], U32, name="bent_words", tag="bent_words", align_bytes=64)
            bent_sc = work.tile([P, CH], U8, name="bent_sc", tag="bent_sc", align_bytes=64)
            nc.vector.quantize_mx(out=bent_words[:].bitcast(FP8X4), scales=bent_sc[:], in_=chunk[c]["bent_bf"][:])
            scores = chunk[c]["scores"]
            for g in range(NT):
                nc.tensor.matmul_mx(
                    out=scores[:, g, :],
                    lhsT=w3_words[:, g * P:(g + 1) * P].bitcast(FP8X4), lhsT_scale=w3_sc[:, g * P:(g + 1) * P],
                    rhs=bent_words[:].bitcast(FP8X4), rhs_scale=bent_sc[:],
                    start=False, stop=(g == NT - 1))
            result = work.tile([P, NT, CH], F32, name="result", tag="result", bufs=4)
            nc.scalar.copy(out=result[:], in_=scores[:])
            nc.sync.dma_start(out=out_v[:, :, c * CH:(c + 1) * CH], in_=result[:])

        chunks = J // CH
        for c in range(chunks):
            passes(c, 0)
        take_larger(last_tile - 1, 0, J)
        pick(last_tile, 0, J // 2)
        weigh(last_tile - 1, 0, J, nc.vector)
        take_larger(last_tile, 0, J // 2)
        pick(last_tile, J // 2, J // 2)
        weigh(last_tile, 0, J // 2, nc.vector)
        weave(1, 0, CH, nc.scalar.copy)
        weave(1, CH, CH, nc.scalar.copy)
        take_larger(last_tile, J // 2, J // 2)
        quantize_worst(1, 0, CH)
        front(0)
        weigh(last_tile, J // 2, J // 2, nc.vector)
        weave(1, 2 * CH, 2 * CH, nc.vector.tensor_copy)
        for c in range(1, chunks):
            quantize_worst(1, c * CH, CH)
            front(c)
        for c in range(chunks + 1):
            if c < chunks:
                bend(c)
            if c > 0:
                back(c - 1)
